import numpy as np
import ml_dtypes


def mxq(x, axis, fmt="e4m3"):
    dtype, down = {"e4m3": (ml_dtypes.float8_e4m3fn, 7), "e5m2": (ml_dtypes.float8_e5m2, 14)}[fmt]
    v = np.moveaxis(np.asarray(x, np.float32).astype(ml_dtypes.bfloat16).astype(np.float64), axis, -1)
    blocks = v.reshape(v.shape[:-1] + (-1, 32))
    amax = np.abs(blocks).max(-1, keepdims=True)
    byte = np.maximum(np.where(amax > 0, np.frexp(amax)[1] - 1 + 127, 0) - down, 1)
    scale = np.exp2(byte - 127.0)
    codes = (blocks / scale).astype(np.float32).astype(dtype).astype(np.float64)
    return np.moveaxis((codes * scale).reshape(v.shape), -1, axis)


WIDE = False


def mx_kscale(k):
    if not WIDE:
        return np.ones(k)
    levels = np.array([10, -10, 5, -5, 0])
    if k % 512:
        return np.exp2(np.random.permutation(np.resize(levels, k // 32))).repeat(32)
    a = np.empty((k // 512, 16))
    for p in range(k // 512):
        a[p, :8] = np.random.permutation(np.resize(levels, 8))
        for g in range(8):
            far = levels[np.abs(levels - a[p, g]) >= 10]
            a[p, g + 8] = far[np.random.randint(len(far))]
    return np.exp2(a.ravel()).repeat(32)


def f64(x):
    return np.asarray(x).astype(np.float64)


def striped(idx):
    return np.tile(np.asarray(idx).reshape(-1, 16).T, (8, 1)).astype(np.uint16)


def unstriped(offs):
    return offs[:16].T.reshape(-1).astype(np.int64)


E2M1 = np.array([0.0, 0.5, 1.0, 1.5, 2.0, 3.0, 4.0, 6.0, -0.0, -0.5, -1.0, -1.5, -2.0, -3.0, -4.0, -6.0])


def pack_weight(w, fmt):
    k, n = w.shape
    w = f64(np.asarray(w, np.float32).astype(ml_dtypes.bfloat16)).reshape(k // 32, 32, n)
    amax = np.abs(w).max(1)
    if fmt == "e4m3":
        byte = np.frexp(amax)[1] - 1 + 127 - 7
    else:
        mant, ex = np.frexp(amax / 6.0)
        byte = np.where(mant > 0.5, ex, ex - 1) + 127
    byte = np.clip(np.where(amax > 0, byte, 1), 1, 254)
    scaled = (w * np.exp2(127.0 - byte)[:, None, :]).reshape(k, n).astype(np.float32)
    by_word = np.ascontiguousarray(scaled.reshape(k // 512, 128, 4, n).transpose(0, 1, 3, 2))
    if fmt == "e4m3":
        words = by_word.astype(ml_dtypes.float8_e4m3fn).view(np.uint8)
    else:
        c = by_word.astype(ml_dtypes.float4_e2m1fn).view(np.uint8) & 0xF
        words = (c[..., 0::2] | (c[..., 1::2] << 4)).reshape(k // 512, 128, 2 * n)
    return np.ascontiguousarray(words), np.ascontiguousarray(byte.astype(np.uint8).reshape(k // 512, 16, n))


def unpack_weight(words, scales, fmt):
    g, _, n = scales.shape
    words = np.ascontiguousarray(words).reshape(g, 128, n, -1)
    if fmt == "e4m3":
        vals = words.view(ml_dtypes.float8_e4m3fn).astype(np.float64)
    else:
        nib = np.empty((g, 128, n, 4), np.uint8)
        nib[..., 0::2] = words & 0xF
        nib[..., 1::2] = words >> 4
        vals = E2M1[nib]
    vals = vals * np.repeat(np.exp2(scales.astype(np.float64) - 127.0), 8, axis=1)[..., None]
    return vals.transpose(0, 1, 3, 2).reshape(g * 512, n)


D, T, I, J, U, Z, E, M = 512, 2048, 512, 512, 1024, 1024, 512, 1024


def setup_inputs():
    n = np.random.standard_normal
    idx = np.random.permutation(T)[:I]
    idx2 = np.random.permutation(U)[:J]
    idx3 = np.random.permutation(Z)[:J]
    idx4 = np.random.permutation(M)[:J]
    fd = mx_kscale(D)
    fi = mx_kscale(I)
    ti = np.ones(T)
    ti[idx] = fi
    keysp = pack_weight(n((D, T)) / fd[:, None], "e4m3")
    return {
        "keys_words": keysp[0],
        "keys_scales": keysp[1],
        "notes": (n((D, U)) * 1.0 / np.sqrt(D) * fd[:, None]).astype(np.float32),
        "given": (np.random.uniform(0.3, 1.7, (I, Z))).astype(np.float32),
        "rowf": (np.random.uniform(0.02, 0.08, (I, 1)) * fi[:, None]).astype(np.float32),
        "vals": (n((E, T)) / ti).astype(np.float32),
        "old": (1.0 * n((E, M))).astype(np.float32),
        "offs": striped(idx),
        "offs2": striped(idx2),
        "offs3": striped(idx3),
        "offs4": striped(idx4),
    }


def reference(keys_words, keys_scales, notes, given, rowf, vals, old, offs, offs2, offs3, offs4):
    idx = unstriped(offs)
    idx2 = unstriped(offs2)
    idx3 = unstriped(offs3)
    idx4 = unstriped(offs4)
    keysu = unpack_weight(keys_words, keys_scales, "e4m3")
    keysidxg = keysu[:, idx]
    notesidx2q = mxq(f64(notes)[:, idx2], 0, "e4m3")
    g1 = keysidxg.T @ notesidx2q
    g0 = g1 * f64(given)[:, idx3]
    gr1 = g0 * f64(rowf)
    vt1 = f64(vals)[:, idx].T
    vt1q = mxq(vt1, 0, "e4m3")
    gr1q = mxq(gr1, 0, "e4m3")
    o = vt1q.T @ gr1q
    of = np.zeros((E, M))
    of[:, idx4] = o
    y = f64(old) + of
    return y

@@ -1,0 +1,191 @@
+from contextlib import ExitStack
+
+import concourse.mybir as mybir
+from concourse.masks import make_identity
+
+D, T, I, J, U, Z, E, M = 512, 2048, 512, 512, 1024, 1024, 512, 1024
+FLOPS = 2 * D * I * J + 2 * I * E * J
+
+F32 = mybir.dt.float32
+BF16 = mybir.dt.bfloat16
+I32 = mybir.dt.int32
+U32 = mybir.dt.uint32
+U16 = mybir.dt.uint16
+U8 = mybir.dt.uint8
+FP8X4 = mybir.dt.float8_e4m3fn_x4
+COPY = mybir.ActivationFunctionType.Copy
+MULT = mybir.AluOpType.mult
+ADD = mybir.AluOpType.add
+
+P = 128
+PACK = 4
+E_TILES = E // P
+HALF = J // 2
+LIST_COLS = J // 16
+
+
+def tile_attend_tab_timestable_put_kernel(
+    tc, keys_words, keys_scales, notes, given, rowf, vals, old, offs, offs2, offs3, offs4, out
+):
+    nc = tc.nc
+    with ExitStack() as ctx:
+        keep = ctx.enter_context(tc.tile_pool(name="keep", bufs=1))
+        psum = ctx.enter_context(tc.psum_pool(name="psum", bufs=1))
+
+        def sb(shape, dtype, name, tag=None):
+            return keep.tile(shape, dtype, name=name, tag=tag or name, align_bytes=64)
+
+        idx = sb([P, LIST_COLS], U16, "idx")
+        idx2 = sb([P, LIST_COLS], U16, "idx2")
+        idx3 = sb([P, LIST_COLS], U16, "idx3")
+        idx4 = sb([P, LIST_COLS], U16, "idx4")
+        notes_sb = [sb([P, U], F32, "notes%d" % t) for t in range(PACK)]
+        given_sb = [sb([P, Z], F32, "given%d" % t) for t in range(PACK)]
+        vals_sb = [sb([P, T], F32, "vals%d" % k) for k in range(E_TILES)]
+        old_sb = [sb([P, M], F32, "old%d" % k) for k in range(E_TILES)]
+        placed = [sb([P, M], F32, "placed%d" % k) for k in range(E_TILES)]
+        kwords = sb([P, T], U32, "kwords")
+        kscales = sb([P, T], U8, "kscales")
+        rowf_sb = sb([P, PACK], F32, "rowf_sb")
+        ident = sb([P, P], F32, "ident")
+
+        notes_planes = notes.rearrange("(p t) u -> p t u", t=PACK)
+        given_planes = given.rearrange("(p t) z -> p t z", t=PACK)
+
+        nc.vector.memset(kscales[:].bitcast(I32), 0)
+        nc.sync.dma_start(notes_sb[0][:], notes_planes[:, 0, :])
+        nc.sync.dma_start(idx2[:], offs2)
+        nc.sync.dma_start(idx[:], offs)
+        for q in range(4):
+            nc.sync.dma_start(
+                kscales[32 * q : 32 * q + 4, :].bitcast(I32), keys_scales[0, 4 * q : 4 * q + 4, :].bitcast(I32)
+            )
+        for t in range(1, PACK):
+            nc.sync.dma_start(notes_sb[t][:], notes_planes[:, t, :])
+        nc.sync.dma_start(kwords[:].bitcast(I32), keys_words[0].rearrange("p n t -> p (n t)").bitcast(I32))
+        nc.sync.dma_start(given_sb[0][:], given_planes[:, 0, :])
+        nc.sync.dma_start(idx3[:], offs3)
+        nc.sync.dma_start(rowf_sb[:], rowf.rearrange("(p t) o -> p (t o)", t=PACK))
+        for t in range(1, PACK):
+            nc.sync.dma_start(given_sb[t][:], given_planes[:, t, :])
+        nc.sync.dma_start(idx4[:], offs4)
+        for k in range(E_TILES):
+            nc.sync.dma_start(vals_sb[k][:], vals[k * P : (k + 1) * P, :])
+        for k in range(E_TILES):
+            nc.sync.dma_start(old_sb[k][:], old[k * P : (k + 1) * P, :])
+
+        make_identity(nc, ident[:])
+        for k in range(E_TILES):
+            nc.gpsimd.memset(placed[k][:], 0.0)
+
+        def interleave(dst, src):
+            nc.vector.tensor_copy(
+                dst[:].rearrange("p (c i t) -> p c t i", i=4, t=PACK),
+                src[:].rearrange("p t (c i) -> p c t i", i=4),
+            )
+
+        kscales_g = sb([P, I], U8, "kscales_g")
+        nc.vector.tensor_copy(kscales_g[:].rearrange("p (t s) -> p s t", t=PACK), kscales[:].indirect(idx[:]))
+
+        notes_g = sb([P, PACK, J], BF16, "notes_g")
+        for t in range(PACK):
+            picked = notes_sb[t][:].indirect(idx2[:])
+            if t < PACK - 1:
+                nc.scalar.activation(notes_g[:, t, :], picked, COPY)
+            else:
+                nc.vector.tensor_copy(notes_g[:, t, :], picked)
+        notes_i = sb([P, J * PACK], BF16, "notes_i")
+        interleave(notes_i, notes_g)
+        notes_q = sb([P, J], U32, "notes_q")
+        notes_s = sb([P, J], U8, "notes_s")
+        nc.vector.quantize_mx(notes_q[:].bitcast(FP8X4), notes_s[:], notes_i[:])
+
+        kwords_g = sb([P, I], U32, "kwords_g")
+        nc.vector.tensor_copy(kwords_g[:].rearrange("p (t s) -> p s t", t=PACK), kwords[:].indirect(idx[:]))
+
+        table_planes = sb([P, PACK, J], BF16, "table_planes")
+        for t in range(PACK):
+            cols = slice(t * P, (t + 1) * P)
+            g1 = psum.tile([P, J], F32, name="g1_%d" % t, tag="g1_%d" % t)
+            nc.tensor.matmul_mx(
+                g1[:], kwords_g[:, cols].bitcast(FP8X4), kscales_g[:, cols], notes_q[:].bitcast(FP8X4), notes_s[:],
+                start=True, stop=True,
+            )
+            given_g = sb([P, J], F32, "given_g%d" % t)
+            nc.scalar.activation(given_g[:], given_sb[t][:].indirect(idx3[:]), COPY)
+            nc.vector.scalar_tensor_tensor(table_planes[:, t, :], g1[:], rowf_sb[:, t : t + 1], given_g[:], MULT, MULT)
+        table_i = sb([P, J * PACK], BF16, "table_i")
+        interleave(table_i, table_planes)
+        table_q = sb([P, J], U32, "table_q")
+        table_s = sb([P, J], U8, "table_s")
+        nc.vector.quantize_mx(table_q[:].bitcast(FP8X4), table_s[:], table_i[:])
+
+        quantised = []
+
+        def prepare(k):
+            vals_g = sb([P, I], BF16, "vals_g%d" % k)
+            nc.scalar.activation(vals_g[:], vals_sb[k][:].indirect(idx[:]), COPY)
+            words = vals_g[:].bitcast(F32)
+            turned = psum.tile([P, 2, P], F32, name="turned%d" % k, tag="turned%d" % (k % 2))
+            for u in range(2):
+                nc.tensor.transpose(turned[:, u, :], words[:, u : 2 * P : 2], ident[:])
+            vals_i = sb([P, P * PACK], BF16, "vals_i%d" % k)
+            nc.scalar.copy(
+                vals_i[:].bitcast(F32).rearrange("p (r u) -> p r u", u=2), turned[:].rearrange("p u r -> p r u")
+            )
+            vals_q = sb([P, P], U32, "vals_q%d" % k)
+            vals_s = sb([P, P], U8, "vals_s%d" % k)
+            nc.vector.quantize_mx(vals_q[:].bitcast(FP8X4), vals_s[:], vals_i[:])
+            quantised.append((vals_q, vals_s))
+
+        def product(k, bank):
+            vals_q, vals_s = quantised[k]
+            o = psum.tile([P, J], F32, name="o%d" % k, tag=bank)
+            nc.tensor.matmul_mx(
+                o[:], vals_q[:].bitcast(FP8X4), vals_s[:], table_q[:].bitcast(FP8X4), table_s[:], start=True, stop=True
+            )
+            return o
+
+        def half(h):
+            return slice(h * HALF, (h + 1) * HALF)
+
+        def window(k, h):
+            return placed[k][:].indirect(idx4[:, h * LIST_COLS // 2 : (h + 1) * LIST_COLS // 2])
+
+        def finish(k, engine, cols):
+            engine.tensor_tensor(old_sb[k][:, cols], old_sb[k][:, cols], placed[k][:, cols], ADD)
+            nc.sync.dma_start(out[k * P : (k + 1) * P, cols], old_sb[k][:, cols])
+
+        prepare(0)
+        o0 = product(0, "g1_0")
+        o0a = sb([P, HALF], F32, "o0a")
+        o0b = sb([P, HALF], F32, "o0b")
+        nc.vector.tensor_copy(o0a[:], o0[:, half(0)])
+        nc.vector.tensor_copy(window(0, 0), o0a[:])
+        prepare(1)
+        nc.scalar.copy(o0b[:], o0[:, half(1)])
+        nc.vector.tensor_copy(window(0, 1), o0b[:])
+        o1 = product(1, "g1_1")
+        prepare(2)
+        o1a = sb([P, HALF], F32, "o1a", "vals_i2")
+        nc.vector.tensor_copy(o1a[:], o1[:, half(0)])
+        nc.vector.tensor_copy(window(1, 0), o1a[:])
+        prepare(3)
+        o1b = sb([P, HALF], F32, "o1b", "vals_g3")
+        nc.scalar.copy(o1b[:], o1[:, half(1)])
+        nc.vector.tensor_copy(window(1, 1), o1b[:])
+        o2 = product(2, "turned1")
+        o3 = product(3, "g1_3")
+        o2_sb = sb([P, J], F32, "o2_sb")
+        nc.scalar.copy(o2_sb[:], o2[:])
+        nc.scalar.activation(window(2, 0), o2_sb[:, half(0)], COPY)
+        nc.vector.tensor_copy(window(2, 1), o2_sb[:, half(1)])
+        o3_sb = sb([P, J], F32, "o3_sb")
+        nc.scalar.copy(o3_sb[:], o3[:])
+        for h in range(2):
+            nc.scalar.activation(window(3, h), o3_sb[:, half(h)], COPY)
+        finish(0, nc.gpsimd, slice(0, M))
+        finish(1, nc.gpsimd, slice(0, M))
+        finish(2, nc.vector, slice(0, M))
+        for h in range(2):
+            finish(3, nc.vector, slice(h * M // 2, (h + 1) * M // 2))

@@ -68,15 +68,16 @@ def tile_attend_tab_timestable_put_kernel(
         nc.sync.dma_start(rowf_sb[:], rowf.rearrange("(p t) o -> p (t o)", t=PACK))
         for t in range(1, PACK):
             nc.sync.dma_start(given_sb[t][:], given_planes[:, t, :])
+        nc.sync.dma_start(vals_sb[0][:], vals[0:P, :])
         nc.sync.dma_start(idx4[:], offs4)
-        for k in range(E_TILES):
+        for k in range(1, E_TILES):
             nc.sync.dma_start(vals_sb[k][:], vals[k * P : (k + 1) * P, :])
         for k in range(E_TILES):
             nc.sync.dma_start(old_sb[k][:], old[k * P : (k + 1) * P, :])
 
         make_identity(nc, ident[:])
         for k in range(E_TILES):
-            nc.gpsimd.memset(placed[k][:], 0.0)
+            nc.vector.memset(placed[k][:], 0.0)
 
         def interleave(dst, src):
             nc.vector.tensor_copy(
@@ -122,70 +123,79 @@ def tile_attend_tab_timestable_put_kernel(
 
         quantised = []
 
-        def prepare(k):
+        def move(on_scalar, dst, src):
+            if on_scalar:
+                nc.scalar.copy(dst, src)
+            else:
+                nc.vector.tensor_copy(dst, src)
+
+        def move_listed(on_scalar, dst, src):
+            if on_scalar:
+                nc.scalar.activation(dst, src, COPY)
+            else:
+                nc.vector.tensor_copy(dst, src)
+
+        def prepare(k, gather_on_scalar, copy_on_scalar):
             vals_g = sb([P, I], BF16, "vals_g%d" % k)
-            nc.scalar.activation(vals_g[:], vals_sb[k][:].indirect(idx[:]), COPY)
+            move_listed(gather_on_scalar, vals_g[:], vals_sb[k][:].indirect(idx[:]))
             words = vals_g[:].bitcast(F32)
             turned = psum.tile([P, 2, P], F32, name="turned%d" % k, tag="turned%d" % (k % 2))
             for u in range(2):
                 nc.tensor.transpose(turned[:, u, :], words[:, u : 2 * P : 2], ident[:])
             vals_i = sb([P, P * PACK], BF16, "vals_i%d" % k)
-            nc.scalar.copy(
-                vals_i[:].bitcast(F32).rearrange("p (r u) -> p r u", u=2), turned[:].rearrange("p u r -> p r u")
+            move(
+                copy_on_scalar,
+                vals_i[:].bitcast(F32).rearrange("p (r u) -> p r u", u=2),
+                turned[:].rearrange("p u r -> p r u"),
             )
             vals_q = sb([P, P], U32, "vals_q%d" % k)
             vals_s = sb([P, P], U8, "vals_s%d" % k)
             nc.vector.quantize_mx(vals_q[:].bitcast(FP8X4), vals_s[:], vals_i[:])
             quantised.append((vals_q, vals_s))
 
-        def product(k, bank):
+        def product(k):
             vals_q, vals_s = quantised[k]
-            o = psum.tile([P, J], F32, name="o%d" % k, tag=bank)
+            o = psum.tile([P, J], F32, name="o%d" % k, tag="g1_%d" % k)
             nc.tensor.matmul_mx(
                 o[:], vals_q[:].bitcast(FP8X4), vals_s[:], table_q[:].bitcast(FP8X4), table_s[:], start=True, stop=True
             )
             return o
 
-        def half(h):
-            return slice(h * HALF, (h + 1) * HALF)
+        def take(k, o, lo, hi, on_scalar, slot):
+            piece = sb([P, hi - lo], F32, "piece%d_%d" % (k, lo), slot)
+            move(on_scalar, piece[:], o[:, lo:hi])
+            return piece
 
-        def window(k, h):
-            return placed[k][:].indirect(idx4[:, h * LIST_COLS // 2 : (h + 1) * LIST_COLS // 2])
+        def put(k, piece, lo, hi, on_scalar):
+            move_listed(on_scalar, placed[k][:].indirect(idx4[:, lo // 16 : hi // 16]), piece)
 
-        def finish(k, engine, cols):
-            engine.tensor_tensor(old_sb[k][:, cols], old_sb[k][:, cols], placed[k][:, cols], ADD)
-            nc.sync.dma_start(out[k * P : (k + 1) * P, cols], old_sb[k][:, cols])
+        def finish(k, engine, cols, slot):
+            res = sb([P, cols.stop - cols.start], F32, "res%d_%d" % (k, cols.start), slot)
+            engine.tensor_tensor(res[:], old_sb[k][:, cols], placed[k][:, cols], ADD)
+            nc.sync.dma_start(out[k * P : (k + 1) * P, cols], res[:])
 
-        prepare(0)
-        o0 = product(0, "g1_0")
-        o0a = sb([P, HALF], F32, "o0a")
-        o0b = sb([P, HALF], F32, "o0b")
-        nc.vector.tensor_copy(o0a[:], o0[:, half(0)])
-        nc.vector.tensor_copy(window(0, 0), o0a[:])
-        prepare(1)
-        nc.scalar.copy(o0b[:], o0[:, half(1)])
-        nc.vector.tensor_copy(window(0, 1), o0b[:])
-        o1 = product(1, "g1_1")
-        prepare(2)
-        o1a = sb([P, HALF], F32, "o1a", "vals_i2")
-        nc.vector.tensor_copy(o1a[:], o1[:, half(0)])
-        nc.vector.tensor_copy(window(1, 0), o1a[:])
-        prepare(3)
-        o1b = sb([P, HALF], F32, "o1b", "vals_g3")
-        nc.scalar.copy(o1b[:], o1[:, half(1)])
-        nc.vector.tensor_copy(window(1, 1), o1b[:])
-        o2 = product(2, "turned1")
-        o3 = product(3, "g1_3")
-        o2_sb = sb([P, J], F32, "o2_sb")
-        nc.scalar.copy(o2_sb[:], o2[:])
-        nc.scalar.activation(window(2, 0), o2_sb[:, half(0)], COPY)
-        nc.vector.tensor_copy(window(2, 1), o2_sb[:, half(1)])
-        o3_sb = sb([P, J], F32, "o3_sb")
-        nc.scalar.copy(o3_sb[:], o3[:])
+        prepare(0, True, True)
+        prepare(1, True, False)
+        o0 = product(0)
+        o0a = take(0, o0, 0, HALF, False, "vals1")
+        o0b = take(0, o0, HALF, J, False, None)
+        put(0, o0a[:], 0, HALF, True)
+        put(0, o0b[:], HALF, J, True)
+        prepare(2, False, False)
+        o1 = take(1, product(1), 0, J, False, "vals2")
+        put(1, o1[:, 0:HALF], 0, HALF, True)
+        put(1, o1[:, HALF:J], HALF, J, True)
+        prepare(3, False, False)
+        o2 = product(2)
+        o2a = take(2, o2, 0, HALF, False, "vals3")
+        put(2, o2a[:], 0, HALF, True)
+        o2b = take(2, o2, HALF, J, False, "vals_i3")
+        o3 = take(3, product(3), 0, J, True, None)
+        put(3, o3[:, 0:HALF], 0, HALF, True)
+        put(3, o3[:, HALF:J], HALF, J, True)
+        finish(0, nc.vector, slice(0, M), "vals_q3")
+        finish(1, nc.vector, slice(0, M), None)
+        put(2, o2b[:], HALF, J, False)
+        finish(2, nc.vector, slice(0, M), None)
         for h in range(2):
-            nc.scalar.activation(window(3, h), o3_sb[:, half(h)], COPY)
-        finish(0, nc.gpsimd, slice(0, M))
-        finish(1, nc.gpsimd, slice(0, M))
-        finish(2, nc.vector, slice(0, M))
-        for h in range(2):
-            finish(3, nc.vector, slice(h * M // 2, (h + 1) * M // 2))
+            finish(3, nc.vector, slice(h * M // 2, (h + 1) * M // 2), None)

@@ -70,9 +70,11 @@ def tile_attend_tab_timestable_put_kernel(
             nc.sync.dma_start(given_sb[t][:], given_planes[:, t, :])
         nc.sync.dma_start(vals_sb[0][:], vals[0:P, :])
         nc.sync.dma_start(idx4[:], offs4)
-        for k in range(1, E_TILES):
+        for k in range(1, E_TILES - 1):
             nc.sync.dma_start(vals_sb[k][:], vals[k * P : (k + 1) * P, :])
-        for k in range(E_TILES):
+        nc.sync.dma_start(old_sb[0][:], old[0:P, :])
+        nc.sync.dma_start(vals_sb[E_TILES - 1][:], vals[E - P : E, :])
+        for k in range(1, E_TILES):
             nc.sync.dma_start(old_sb[k][:], old[k * P : (k + 1) * P, :])
 
         make_identity(nc, ident[:])
@@ -104,7 +106,13 @@ def tile_attend_tab_timestable_put_kernel(
         kwords_g = sb([P, I], U32, "kwords_g")
         nc.vector.tensor_copy(kwords_g[:].rearrange("p (t s) -> p s t", t=PACK), kwords[:].indirect(idx[:]))
 
-        table_planes = sb([P, PACK, J], BF16, "table_planes")
+        given_g = [sb([P, J], F32, "given_g%d" % t) for t in range(PACK)]
+        for t in range(PACK):
+            if t == 1:
+                nc.vector.tensor_copy(given_g[t][:], given_sb[t][:].indirect(idx3[:]))
+            else:
+                nc.scalar.activation(given_g[t][:], given_sb[t][:].indirect(idx3[:]), COPY)
+        table_planes = sb([P, PACK, J], BF16, "table_planes", "given1")
         for t in range(PACK):
             cols = slice(t * P, (t + 1) * P)
             g1 = psum.tile([P, J], F32, name="g1_%d" % t, tag="g1_%d" % t)
@@ -112,9 +120,9 @@ def tile_attend_tab_timestable_put_kernel(
                 g1[:], kwords_g[:, cols].bitcast(FP8X4), kscales_g[:, cols], notes_q[:].bitcast(FP8X4), notes_s[:],
                 start=True, stop=True,
             )
-            given_g = sb([P, J], F32, "given_g%d" % t)
-            nc.scalar.activation(given_g[:], given_sb[t][:].indirect(idx3[:]), COPY)
-            nc.vector.scalar_tensor_tensor(table_planes[:, t, :], g1[:], rowf_sb[:, t : t + 1], given_g[:], MULT, MULT)
+            nc.vector.scalar_tensor_tensor(
+                table_planes[:, t, :], g1[:], rowf_sb[:, t : t + 1], given_g[t][:], MULT, MULT
+            )
         table_i = sb([P, J * PACK], BF16, "table_i")
         interleave(table_i, table_planes)
         table_q = sb([P, J], U32, "table_q")
@@ -135,35 +143,39 @@ def tile_attend_tab_timestable_put_kernel(
             else:
                 nc.vector.tensor_copy(dst, src)
 
-        def prepare(k, gather_on_scalar, copy_on_scalar):
+        def gather(k, on_scalar):
             vals_g = sb([P, I], BF16, "vals_g%d" % k)
-            move_listed(gather_on_scalar, vals_g[:], vals_sb[k][:].indirect(idx[:]))
+            move_listed(on_scalar, vals_g[:], vals_sb[k][:].indirect(idx[:]))
+            return vals_g
+
+        def prepare(k, vals_g, bank, slot, codes_slot=None):
             words = vals_g[:].bitcast(F32)
-            turned = psum.tile([P, 2, P], F32, name="turned%d" % k, tag="turned%d" % (k % 2))
+            turned = psum.tile([P, 2, P], F32, name="turned%d" % k, tag=bank)
             for u in range(2):
                 nc.tensor.transpose(turned[:, u, :], words[:, u : 2 * P : 2], ident[:])
-            vals_i = sb([P, P * PACK], BF16, "vals_i%d" % k)
+            vals_i = sb([P, P * PACK], BF16, "vals_i%d" % k, slot)
             move(
-                copy_on_scalar,
+                k == 0,
                 vals_i[:].bitcast(F32).rearrange("p (r u) -> p r u", u=2),
                 turned[:].rearrange("p u r -> p r u"),
             )
-            vals_q = sb([P, P], U32, "vals_q%d" % k)
+            vals_q = sb([P, P], U32, "vals_q%d" % k, codes_slot)
             vals_s = sb([P, P], U8, "vals_s%d" % k)
             nc.vector.quantize_mx(vals_q[:].bitcast(FP8X4), vals_s[:], vals_i[:])
             quantised.append((vals_q, vals_s))
 
-        def product(k):
+        def product(k, lo, hi, bank):
             vals_q, vals_s = quantised[k]
-            o = psum.tile([P, J], F32, name="o%d" % k, tag="g1_%d" % k)
+            o = psum.tile([P, hi - lo], F32, name="o%d_%d" % (k, lo), tag=bank)
             nc.tensor.matmul_mx(
-                o[:], vals_q[:].bitcast(FP8X4), vals_s[:], table_q[:].bitcast(FP8X4), table_s[:], start=True, stop=True
+                o[:], vals_q[:].bitcast(FP8X4), vals_s[:], table_q[:, lo:hi].bitcast(FP8X4), table_s[:, lo:hi],
+                start=True, stop=True,
             )
             return o
 
-        def take(k, o, lo, hi, on_scalar, slot):
-            piece = sb([P, hi - lo], F32, "piece%d_%d" % (k, lo), slot)
-            move(on_scalar, piece[:], o[:, lo:hi])
+        def take(name, sums, slot):
+            piece = sb([P, sums.shape[1]], F32, name, slot)
+            nc.vector.tensor_copy(piece[:], sums)
             return piece
 
         def put(k, piece, lo, hi, on_scalar):
@@ -174,28 +186,37 @@ def tile_attend_tab_timestable_put_kernel(
             engine.tensor_tensor(res[:], old_sb[k][:, cols], placed[k][:, cols], ADD)
             nc.sync.dma_start(out[k * P : (k + 1) * P, cols], res[:])
 
-        prepare(0, True, True)
-        prepare(1, True, False)
-        o0 = product(0)
-        o0a = take(0, o0, 0, HALF, False, "vals1")
-        o0b = take(0, o0, HALF, J, False, None)
-        put(0, o0a[:], 0, HALF, True)
-        put(0, o0b[:], HALF, J, True)
-        prepare(2, False, False)
-        o1 = take(1, product(1), 0, J, False, "vals2")
-        put(1, o1[:, 0:HALF], 0, HALF, True)
-        put(1, o1[:, HALF:J], HALF, J, True)
-        prepare(3, False, False)
-        o2 = product(2)
-        o2a = take(2, o2, 0, HALF, False, "vals3")
-        put(2, o2a[:], 0, HALF, True)
-        o2b = take(2, o2, HALF, J, False, "vals_i3")
-        o3 = take(3, product(3), 0, J, True, None)
-        put(3, o3[:, 0:HALF], 0, HALF, True)
-        put(3, o3[:, HALF:J], HALF, J, True)
-        finish(0, nc.vector, slice(0, M), "vals_q3")
-        finish(1, nc.vector, slice(0, M), None)
+        prepare(0, gather(0, True), "turned", None, "table_i")
+        o0a_sums = product(0, 0, HALF, "g1_0")
+        o0b_sums = product(0, HALF, J, "g1_1")
+        vals_g1 = gather(1, True)
+        o0 = sb([P, J], F32, "o0", "vals1")
+        nc.vector.tensor_copy(o0[:, 0:HALF], o0a_sums[:])
+        nc.vector.tensor_copy(o0[:, HALF:J], o0b_sums[:])
+        put(0, o0[:, 0:HALF], 0, HALF, True)
+        put(0, o0[:, HALF:J], HALF, J, True)
+        vals_g2 = gather(2, False)
+        prepare(1, vals_g1, "g1_0", "vals2")
+        o1_sums = product(1, 0, J, "g1_2")
+        o1 = sb([P, J], F32, "o1")
+        for lo in (0, HALF):
+            nc.scalar.copy(o1[:, lo : lo + HALF], o1_sums[:, lo : lo + HALF])
+            put(1, o1[:, lo : lo + HALF], lo, lo + HALF, True)
+        prepare(2, vals_g2, "turned", None)
+        o2_sums = product(2, 0, J, "g1_3")
+        finish(0, nc.gpsimd, slice(0, M), "vals_i2")
+        prepare(3, gather(3, False), "turned", None)
+        o3_sums = product(3, 0, J, "g1_1")
+        o2a = take("o2a", o2_sums[:, 0:HALF], "vals_i3")
+        o3a = take("o3a", o3_sums[:, 0:HALF], None)
+        o2b = take("o2b", o2_sums[:, HALF:J], "vals_q3")
         put(2, o2b[:], HALF, J, False)
-        finish(2, nc.vector, slice(0, M), None)
-        for h in range(2):
-            finish(3, nc.vector, slice(h * M // 2, (h + 1) * M // 2), None)
+        put(2, o2a[:], 0, HALF, False)
+        put(3, o3a[:], 0, HALF, True)
+        o3b = sb([P, HALF], F32, "o3b")
+        nc.scalar.copy(o3b[:], o3_sums[:, HALF:J])
+        put(3, o3b[:], HALF, J, True)
+        finish(1, nc.gpsimd, slice(0, M), None)
+        for k in (2, 3):
+            for h in range(2):
+                finish(k, nc.vector, slice(h * M // 2, (h + 1) * M // 2), None)

@@ -70,11 +70,9 @@ def tile_attend_tab_timestable_put_kernel(
             nc.sync.dma_start(given_sb[t][:], given_planes[:, t, :])
         nc.sync.dma_start(vals_sb[0][:], vals[0:P, :])
         nc.sync.dma_start(idx4[:], offs4)
-        for k in range(1, E_TILES - 1):
-            nc.sync.dma_start(vals_sb[k][:], vals[k * P : (k + 1) * P, :])
-        nc.sync.dma_start(old_sb[0][:], old[0:P, :])
-        nc.sync.dma_start(vals_sb[E_TILES - 1][:], vals[E - P : E, :])
         for k in range(1, E_TILES):
+            nc.sync.dma_start(vals_sb[k][:], vals[k * P : (k + 1) * P, :])
+        for k in range(E_TILES):
             nc.sync.dma_start(old_sb[k][:], old[k * P : (k + 1) * P, :])
 
         make_identity(nc, ident[:])
@@ -204,10 +202,11 @@ def tile_attend_tab_timestable_put_kernel(
             put(1, o1[:, lo : lo + HALF], lo, lo + HALF, True)
         prepare(2, vals_g2, "turned", None)
         o2_sums = product(2, 0, J, "g1_3")
-        finish(0, nc.gpsimd, slice(0, M), "vals_i2")
-        prepare(3, gather(3, False), "turned", None)
+        vals_g3 = gather(3, False)
+        o2a = take("o2a", o2_sums[:, 0:HALF], "vals3")
+        prepare(3, vals_g3, "turned", None)
+        finish(0, nc.gpsimd, slice(0, M), "vals_i3")
         o3_sums = product(3, 0, J, "g1_1")
-        o2a = take("o2a", o2_sums[:, 0:HALF], "vals_i3")
         o3a = take("o3a", o3_sums[:, 0:HALF], None)
         o2b = take("o2b", o2_sums[:, HALF:J], "vals_q3")
         put(2, o2b[:], HALF, J, False)

from contextlib import ExitStack

import concourse.mybir as mybir
from concourse.masks import make_identity

D, T, I, J, U, Z, E, M = 512, 2048, 512, 512, 1024, 1024, 512, 1024
FLOPS = 2 * D * I * J + 2 * I * E * J

F32 = mybir.dt.float32
BF16 = mybir.dt.bfloat16
I32 = mybir.dt.int32
U32 = mybir.dt.uint32
U16 = mybir.dt.uint16
U8 = mybir.dt.uint8
FP8X4 = mybir.dt.float8_e4m3fn_x4
COPY = mybir.ActivationFunctionType.Copy
MULT = mybir.AluOpType.mult
ADD = mybir.AluOpType.add

P = 128
PACK = 4
E_TILES = E // P
HALF = J // 2
LIST_COLS = J // 16


def tile_attend_tab_timestable_put_kernel(
    tc, keys_words, keys_scales, notes, given, rowf, vals, old, offs, offs2, offs3, offs4, out
):
    nc = tc.nc
    with ExitStack() as ctx:
        keep = ctx.enter_context(tc.tile_pool(name="keep", bufs=1))
        psum = ctx.enter_context(tc.psum_pool(name="psum", bufs=1))

        def sb(shape, dtype, name, tag=None):
            return keep.tile(shape, dtype, name=name, tag=tag or name, align_bytes=64)

        idx = sb([P, LIST_COLS], U16, "idx")
        idx2 = sb([P, LIST_COLS], U16, "idx2")
        idx3 = sb([P, LIST_COLS], U16, "idx3")
        idx4 = sb([P, LIST_COLS], U16, "idx4")
        notes_sb = [sb([P, U], F32, "notes%d" % t) for t in range(PACK)]
        given_sb = [sb([P, Z], F32, "given%d" % t) for t in range(PACK)]
        vals_sb = [sb([P, T], F32, "vals%d" % k) for k in range(E_TILES)]
        old_sb = [sb([P, M], F32, "old%d" % k) for k in range(E_TILES)]
        placed = [sb([P, M], F32, "placed%d" % k) for k in range(E_TILES)]
        kwords = sb([P, T], U32, "kwords")
        kscales = sb([P, T], U8, "kscales")
        rowf_sb = sb([P, PACK], F32, "rowf_sb")
        ident = sb([P, P], F32, "ident")

        notes_planes = notes.rearrange("(p t) u -> p t u", t=PACK)
        given_planes = given.rearrange("(p t) z -> p t z", t=PACK)

        nc.vector.memset(kscales[:].bitcast(I32), 0)
        nc.sync.dma_start(notes_sb[0][:], notes_planes[:, 0, :])
        nc.sync.dma_start(idx2[:], offs2)
        nc.sync.dma_start(idx[:], offs)
        for q in range(4):
            nc.sync.dma_start(
                kscales[32 * q : 32 * q + 4, :].bitcast(I32), keys_scales[0, 4 * q : 4 * q + 4, :].bitcast(I32)
            )
        for t in range(1, PACK):
            nc.sync.dma_start(notes_sb[t][:], notes_planes[:, t, :])
        nc.sync.dma_start(kwords[:].bitcast(I32), keys_words[0].rearrange("p n t -> p (n t)").bitcast(I32))
        nc.sync.dma_start(given_sb[0][:], given_planes[:, 0, :])
        nc.sync.dma_start(idx3[:], offs3)
        nc.sync.dma_start(rowf_sb[:], rowf.rearrange("(p t) o -> p (t o)", t=PACK))
        for t in range(1, PACK):
            nc.sync.dma_start(given_sb[t][:], given_planes[:, t, :])
        nc.sync.dma_start(vals_sb[0][:], vals[0:P, :])
        nc.sync.dma_start(idx4[:], offs4)
        for k in range(1, E_TILES):
            nc.sync.dma_start(vals_sb[k][:], vals[k * P : (k + 1) * P, :])
        for k in range(E_TILES):
            nc.sync.dma_start(old_sb[k][:], old[k * P : (k + 1) * P, :])

        make_identity(nc, ident[:])
        for k in range(E_TILES):
            nc.vector.memset(placed[k][:], 0.0)

        def interleave(dst, src):
            nc.vector.tensor_copy(
                dst[:].rearrange("p (c i t) -> p c t i", i=4, t=PACK),
                src[:].rearrange("p t (c i) -> p c t i", i=4),
            )

        kscales_g = sb([P, I], U8, "kscales_g")
        nc.vector.tensor_copy(kscales_g[:].rearrange("p (t s) -> p s t", t=PACK), kscales[:].indirect(idx[:]))

        notes_g = sb([P, PACK, J], BF16, "notes_g")
        for t in range(PACK):
            picked = notes_sb[t][:].indirect(idx2[:])
            if t < PACK - 1:
                nc.scalar.activation(notes_g[:, t, :], picked, COPY)
            else:
                nc.vector.tensor_copy(notes_g[:, t, :], picked)
        notes_i = sb([P, J * PACK], BF16, "notes_i")
        interleave(notes_i, notes_g)
        notes_q = sb([P, J], U32, "notes_q")
        notes_s = sb([P, J], U8, "notes_s")
        nc.vector.quantize_mx(notes_q[:].bitcast(FP8X4), notes_s[:], notes_i[:])

        kwords_g = sb([P, I], U32, "kwords_g")
        nc.vector.tensor_copy(kwords_g[:].rearrange("p (t s) -> p s t", t=PACK), kwords[:].indirect(idx[:]))

        given_g = [sb([P, J], F32, "given_g%d" % t) for t in range(PACK)]
        for t in range(PACK):
            if t == 1:
                nc.vector.tensor_copy(given_g[t][:], given_sb[t][:].indirect(idx3[:]))
            else:
                nc.scalar.activation(given_g[t][:], given_sb[t][:].indirect(idx3[:]), COPY)
        table_planes = sb([P, PACK, J], BF16, "table_planes", "given1")
        for t in range(PACK):
            cols = slice(t * P, (t + 1) * P)
            g1 = psum.tile([P, J], F32, name="g1_%d" % t, tag="g1_%d" % t)
            nc.tensor.matmul_mx(
                g1[:], kwords_g[:, cols].bitcast(FP8X4), kscales_g[:, cols], notes_q[:].bitcast(FP8X4), notes_s[:],
                start=True, stop=True,
            )
            nc.vector.scalar_tensor_tensor(
                table_planes[:, t, :], g1[:], rowf_sb[:, t : t + 1], given_g[t][:], MULT, MULT
            )
        table_i = sb([P, J * PACK], BF16, "table_i")
        interleave(table_i, table_planes)
        table_q = sb([P, J], U32, "table_q")
        table_s = sb([P, J], U8, "table_s")
        nc.vector.quantize_mx(table_q[:].bitcast(FP8X4), table_s[:], table_i[:])

        quantised = []

        def move(on_scalar, dst, src):
            if on_scalar:
                nc.scalar.copy(dst, src)
            else:
                nc.vector.tensor_copy(dst, src)

        def move_listed(on_scalar, dst, src):
            if on_scalar:
                nc.scalar.activation(dst, src, COPY)
            else:
                nc.vector.tensor_copy(dst, src)

        def gather(k, on_scalar):
            vals_g = sb([P, I], BF16, "vals_g%d" % k)
            move_listed(on_scalar, vals_g[:], vals_sb[k][:].indirect(idx[:]))
            return vals_g

        def prepare(k, vals_g, bank, slot, codes_slot=None):
            words = vals_g[:].bitcast(F32)
            turned = psum.tile([P, 2, P], F32, name="turned%d" % k, tag=bank)
            for u in range(2):
                nc.tensor.transpose(turned[:, u, :], words[:, u : 2 * P : 2], ident[:])
            vals_i = sb([P, P * PACK], BF16, "vals_i%d" % k, slot)
            move(
                k == 0,
                vals_i[:].bitcast(F32).rearrange("p (r u) -> p r u", u=2),
                turned[:].rearrange("p u r -> p r u"),
            )
            vals_q = sb([P, P], U32, "vals_q%d" % k, codes_slot)
            vals_s = sb([P, P], U8, "vals_s%d" % k)
            nc.vector.quantize_mx(vals_q[:].bitcast(FP8X4), vals_s[:], vals_i[:])
            quantised.append((vals_q, vals_s))

        def product(k, lo, hi, bank):
            vals_q, vals_s = quantised[k]
            o = psum.tile([P, hi - lo], F32, name="o%d_%d" % (k, lo), tag=bank)
            nc.tensor.matmul_mx(
                o[:], vals_q[:].bitcast(FP8X4), vals_s[:], table_q[:, lo:hi].bitcast(FP8X4), table_s[:, lo:hi],
                start=True, stop=True,
            )
            return o

        def take(name, sums, slot):
            piece = sb([P, sums.shape[1]], F32, name, slot)
            nc.vector.tensor_copy(piece[:], sums)
            return piece

        def put(k, piece, lo, hi, on_scalar):
            move_listed(on_scalar, placed[k][:].indirect(idx4[:, lo // 16 : hi // 16]), piece)

        def finish(k, engine, cols, slot):
            res = sb([P, cols.stop - cols.start], F32, "res%d_%d" % (k, cols.start), slot)
            engine.tensor_tensor(res[:], old_sb[k][:, cols], placed[k][:, cols], ADD)
            nc.sync.dma_start(out[k * P : (k + 1) * P, cols], res[:])

        prepare(0, gather(0, True), "turned", None, "table_i")
        o0a_sums = product(0, 0, HALF, "g1_0")
        o0b_sums = product(0, HALF, J, "g1_1")
        vals_g1 = gather(1, True)
        o0 = sb([P, J], F32, "o0", "vals1")
        nc.vector.tensor_copy(o0[:, 0:HALF], o0a_sums[:])
        nc.vector.tensor_copy(o0[:, HALF:J], o0b_sums[:])
        put(0, o0[:, 0:HALF], 0, HALF, True)
        put(0, o0[:, HALF:J], HALF, J, True)
        vals_g2 = gather(2, False)
        prepare(1, vals_g1, "g1_0", "vals2")
        o1_sums = product(1, 0, J, "g1_2")
        o1 = sb([P, J], F32, "o1")
        for lo in (0, HALF):
            nc.scalar.copy(o1[:, lo : lo + HALF], o1_sums[:, lo : lo + HALF])
            put(1, o1[:, lo : lo + HALF], lo, lo + HALF, True)
        prepare(2, vals_g2, "turned", None)
        o2_sums = product(2, 0, J, "g1_3")
        vals_g3 = gather(3, False)
        o2a = take("o2a", o2_sums[:, 0:HALF], "vals3")
        prepare(3, vals_g3, "turned", None)
        finish(0, nc.gpsimd, slice(0, M), "vals_i3")
        o3_sums = product(3, 0, J, "g1_1")
        o3a = take("o3a", o3_sums[:, 0:HALF], None)
        o2b = take("o2b", o2_sums[:, HALF:J], "vals_q3")
        put(2, o2b[:], HALF, J, False)
        put(2, o2a[:], 0, HALF, False)
        put(3, o3a[:], 0, HALF, True)
        o3b = sb([P, HALF], F32, "o3b")
        nc.scalar.copy(o3b[:], o3_sums[:, HALF:J])
        put(3, o3b[:], HALF, J, True)
        finish(1, nc.gpsimd, slice(0, M), None)
        for k in (2, 3):
            for h in range(2):
                finish(k, nc.vector, slice(h * M // 2, (h + 1) * M // 2), None)
